import numpy as np, ml_dtypes
CORES = [3,11,19,27,35,43,51,59]
N = 8
BF = ml_dtypes.bfloat16
W, V, Q, S, RO = 3072, 384, 3, 3, 3
RK = np.arange(N)[:, None, None]; GR = np.arange(8)[None, :, None]; VE = np.arange(V)[None, None, :]
def unfold(a, m):
    return np.ascontiguousarray(a.reshape(N, 8, 16, m).transpose(0, 1, 3, 2))
def fold(a):
    return np.ascontiguousarray(a.transpose(0, 1, 3, 2)).reshape(N, 128, -1)
def pack(T, U, P, x):
    return {"tx": fold(T).astype(np.float32).astype(BF), "pu": fold(U).astype(np.int32), "p0": fold(P).astype(np.int32), "x0": fold(x).astype(np.float32).astype(BF)}
def pair(rng, P):
    m = rng.integers(0, 17, (N, 8, V // 2, 1))
    P[:, :, 1::2] = np.where(np.arange(16) < m, P[:, :, 0::2], P[:, :, 1::2])
    return P
def parts(rng):
    T = rng.integers(0, 128, (N, 8, W, 16)); U = rng.integers(0, W, (N, 8, W, 16))
    U = np.where(rng.random((N, 8, W, 1)) < 0.25, U[..., :1], U)
    P = rng.integers(0, W, (N, 8, V, 16))
    for k in range(1, 16):
        nxt = U[RK, GR, P[..., k - 1], rng.integers(0, 16, (N, 8, V))]
        P[..., k] = np.where(rng.random((N, 8, V)) < 0.5, nxt, P[..., k])
    P = pair(rng, P)
    near = np.clip(T[RK, GR, P[..., 15]] + rng.integers(-20, 21, (N, 8, V, 16)), 0, 127)
    x = np.where(rng.random((N, 8, V, 1)) < 0.5, near, rng.integers(0, 128, (N, 8, V, 16)))
    return T, U, P, x
def setup_inputs(rng):
    return pack(*parts(rng))
def setup_inputs_ties(rng):
    T, U, P, x = parts(rng)
    few = rng.integers(0, 128, (N, 8, 6, 16)); few[:, :, 0] = 0; few[:, :, 1] = 127
    T = few[RK, GR, rng.integers(0, 6, (N, 8, W))]; x = few[RK, GR, rng.integers(0, 6, (N, 8, V))]
    return pack(T, U, P, x)
def setup_inputs_cuts(rng):
    T, U, P, x = parts(rng); h = W // 2; s = V // 4
    for g in range(8):
        o = rng.permutation(W); P[:, g] = o[h + P[:, g] % h]
        for j in range(s):
            m = (1, Q - 1, Q, N)[j if j < 4 else int(rng.integers(0, 4))]
            nm = o[s + np.arange(N)]; nm[rng.permutation(N)[:m]] = o[j]
            P[:, g, 2 * j + 1] = P[:, g, 2 * j]; P[:, g, 2 * j:2 * j + 2, 15] = nm[:, None]
    return pack(T, U, P, x)
def setup_inputs_crowd(rng):
    T, U, P, x = parts(rng); h = V // 2; r = np.arange(N)[:, None]; j = np.arange(h)[None, :]
    for g in (0, 1, 2, 3, 4, 5, 7):
        o = rng.permutation(W); nm = np.repeat(o[1:N + 1, None], V, axis=1); n = N + 1
        if g in (0, 7):
            if g == 7: o = np.concatenate([np.array([W - 1]), rng.permutation(W - 1)])
            nm = np.stack([rng.permutation(o[i * V:(i + 1) * V]) for i in np.minimum(rng.permutation(N) // Q, N // Q - 1)]); n = (N // Q) * V
        elif g in (1, 4):
            o = 1 + rng.permutation(W - 1); n = ((N - 1) // (Q - 1) + 1) * h
            nm = o[(rng.permutation(N) // (Q - 1))[:, None] * h + np.arange(V)[None, :] // 2]
        elif g == 2: nm[rng.permutation(N)[:Q]] = o[0]
        elif g == 5:
            s = int(rng.integers(0, N - Q + 1)); nm[s:s + Q - 1, :192] = o[0]; nm = nm[:, rng.permutation(V)]
        else: o = np.arange(W)[::-1]; n = 512
        a, b = o[:n], o[n:]
        T[:, g] = T[:, g] >> 2; x[:, g] = x[:, g] >> 2; T[:, g, a] = T[:, g, a] + 96
        P[:, g] = b[P[:, g] % len(b)]; U[:, g] = b[U[:, g] % len(b)]; P[:, g, 1::2] = np.array(P[:, g, 0::2])
        if g == 3:
            m = rng.integers(1, 15, (N, h)); c = W - 512 + 4 * rng.integers(0, 128, (N, h))
            P[r, g, 2 * j, m] = c; P[r, g, 2 * j + 1, m] = c + 1
        else: P[:, g, :, 15] = nm
        if g in (0, 7): P[:, g, :, 14] = np.array(P[:1, g, :, 14]); U[:, g] = np.array(U[:1, g, :, :1])
    return pack(T, U, P, x)
def setup_inputs_few(rng):
    T, U, P, x = parts(rng)
    for g in (0, 2, 4, 6):
        a = np.concatenate([np.array([0, W - 1]), rng.integers(0, W, 10)]); P[:, g] = a[P[:, g] % 12]
        if g in (0, 4): U[:, g] = a[U[:, g] % 12]
    P[:, 2] = np.array(P[:, 2, :, :1]); U[:, 4, ::2] = rng.integers(0, W, (N, W // 2, 16)); U[:, 6] = np.arange(W)[:, None]
    return pack(T, U, P, x)
def setup_inputs_spread(rng):
    T = np.minimum((np.exp2(7 * rng.random((N, 8, W, 1))) * rng.random((N, 8, W, 16))).astype(np.int64), 127)
    x = np.minimum((np.exp2(7 * rng.random((N, 8, V, 1))) * rng.random((N, 8, V, 16))).astype(np.int64), 127)
    U = np.minimum((W * rng.random((N, 8, W, 16)) ** 2).astype(np.int64), W - 1)
    P = np.minimum((W * rng.random((N, 8, V, 16)) ** 3).astype(np.int64), W - 1)
    return pack(T, U, pair(rng, P), x)
def check_inputs(d):
    bad = []
    for k, hi in (("tx", 127), ("pu", W - 1), ("p0", W - 1), ("x0", 127)):
        a = np.asarray(d[k]).astype(np.float64)
        if not (np.all(a >= 0) and np.all(a <= hi)): bad.append("range of " + k)
        elif np.any(np.floor(a) != a): bad.append("whole numbers of " + k)
    return bad
def reference(tx, pu, p0, x0):
    T = unfold(tx.astype(np.float32).astype(np.int32), W); U = unfold(pu.astype(np.int64), W)
    P = unfold(p0.astype(np.int64), V); x = unfold(x0.astype(np.float32).astype(np.int32), V)
    row = np.arange(16); cut = np.zeros((8, W), bool); R4 = RK[..., None]; G4 = GR[..., None]
    for rnd in range(RO):
        d = np.add.reduce(np.abs(T[R4, G4, P] - x[:, :, :, None, :]), axis=4)
        differ = P != P[:, :, np.arange(V) ^ 1]
        q = np.where(np.any(differ, axis=3), np.argmax(differ, axis=3), 15)
        f = np.argmax(np.where(row >= np.maximum(q, 1)[..., None], d, -1), axis=3)
        old = cut[G4, P] & (row >= 1)
        k = np.where(np.any(old, axis=3), np.argmax(old, axis=3), f)
        charged = np.zeros((N, 8, W), bool); charged[RK, GR, P[RK, GR, VE, f]] = True
        cut = cut | (np.add.reduce(charged.astype(np.int64), axis=0) >= Q)
        T[:, cut] = 256
        pup = U[RK, GR, P[RK, GR, VE, k - 1]]
        e = np.add.reduce(np.abs(T[R4, G4, pup] - x[:, :, :, None, :]), axis=4)
        b = np.argmin(e, axis=3); best = pup[RK, GR, VE, b]
        take = e[RK, GR, VE, b] < d[RK, GR, VE, k]
        P[RK, GR, VE, k] = np.where(take, best, P[RK, GR, VE, k])
        x = np.where(take[..., None], (x + T[RK, GR, best]) >> 1, x)
        if rnd + 1 < RO: P = np.roll(P, S, axis=0); x = np.roll(x, S, axis=0)
    return {"yp": fold(P).astype(np.float32), "yx": fold(x).astype(np.float32).astype(BF), "yc": np.repeat(cut[None], N, axis=0).astype(np.float32)}

from concourse.bass import DstId, RemoteDMATransfer
from concourse.mybir import dt, AluOpType, ActivationFunctionType

A = AluOpType
F = ActivationFunctionType
NR, W, V, RO, STEP = 8, 3072, 384, 3, 3
BIG = 1048576.0
NG = 3
UPD = (0, 1, 0, 1, 0, 1)

f, b, i, u = "float32", "bfloat16", "int32", "uint16"
SB = {
    "TX": (b, W), "PU": (i, W), "PI": (i, V), "CU": (u, V), "CD": (f, V), "ONK": (b, V), "YP": (f, V), "YX": (b, V),
    "ONE": (b, 1536), "IDB": (b, 128), "IDF": (f, 128), "IDH": (b, 128), "BO": (b, 128), "BOF": (f, 128), "BO4": (b, 128),
    "BM": (b, 8), "BG": (b, 8), "XT": (b, 8, 32), "CK": (b, 8, 32), "CE": (b, 8, 32), "CP": (b, 8, 32), "TRI": (b, 8, 32),
    "IOI": (i, 128), "MASK": (f, 128), "EX": (b, 1536), "IOM": (b, 128), "IOL": (b, 24), "ZER": (b, 128), "RSK": (f, 256),
    "RSE": (f, 256), "FA": (b, 96), "FB": (b, 96), "CNI": (i, 128), "YC": (f, 2, 128), "YCA": (b, 2, 128),
    "OX": (b, RO * V), "OP": (u, RO * V), "PK": (b, RO * 96), "TH": (f, 24),
}
for n in range(RO):
    SB.update({"LP%d" % n: (u, V), "LX%d" % n: (b, V), "FL%d" % n: (b, 8, 96), "NC%d" % n: (b, 2, 128)})
for n in range(NG):
    SB["G%d" % n] = (b, 2048)
TWO = {"PF": (f, V), "M": (b, 2048), "SP": (f, 128), "SQ": (f, 128), "MK": (f, 128), "LB": (f, 8), "CI": (i, 8),
       "CF": (f, 8), "OL": (b, 8, 24), "OM": (b, 8, 24), "OH": (b, 8, 128), "PL": (u, 8), "OB": (b, 128), "DX": (b, 128),
       "DY": (b, 128), "UU": (f, 128), "WI": (i, 128)}
THREE = {"DF": (b, 128), "DZ": (f, 256), "PM": (f, 256), "SC": (f, 272), "OT": (b, 8, 32), "OF": (b, 136), "OK": (b, 136),
         "SK": (f, 272), "AJ": (f, 256)}
for n, s in TWO.items():
    SB.update({n + "0": s, n + "1": s})
for n, s in THREE.items():
    SB.update({n + "0": s, n + "1": s, n + "2": s})
SCRATCH = {n: ("sbuf", [128] + list(s[1:]), s[0]) for n, s in SB.items()}
BANKS = {"XR0": [512], "XR1": [512], "K0": [512], "K1": [512], "K2": [512], "PA": [512], "PB": [512], "HI": [8, 24]}
SCRATCH.update({n: ("psum", [128] + s, f) for n, s in BANKS.items()})
SEMAPHORES = ["cv", "cs", "cp", "cg", "loc"] + ["d%d" % n for n in range(16)] + ["fl%d" % n for n in range(RO)] + \
    ["a%d%d" % (s, n) for s in range(RO - 1) for n in range(3)]


def make_plan(g, T):
    eng = {"v": g.vector, "s": g.scalar, "p": g.tensor, "g": g, "y": g.sync}
    nodes = []
    wr, rd, touch, last = {}, {}, {}, {}

    def add(e, reads, writes, emit, sem, inc, cost, acc=False, lag=0.1, own=True, after=()):
        deps, me = set(after), len(nodes)
        bks = sorted(set(k.split(":")[0] for k in list(reads) + list(writes) if k.split(":")[0] in BANKS))
        for bk in bks:
            h = touch.setdefault(bk, [e, [], []])
            if h[0] != e:
                h[:] = [e, [], h[1]]
            deps.update(h[2])
            h[1].append(me)
        for k in reads:
            if k in wr:
                deps.add(wr[k])
        for k in writes:
            if not acc:
                if k in wr:
                    deps.add(wr[k])
                deps.update(rd.get(k, ()))
        nodes.append({"e": e, "deps": sorted(deps), "emit": emit, "sem": sem, "inc": inc, "cost": cost, "lag": lag, "own": own})
        if e == "p":
            for bk in bks:
                if bk in last:
                    nodes[me]["prev"] = last[bk]
                last[bk] = me
        for k in reads:
            rd.setdefault(k, []).append(me)
        for k in writes:
            wr[k] = me
            rd[k] = []
        return me

    fns = {"mm": ("p", g.tensor.matmul), "tt": ("v", g.vector.tensor_tensor), "ts": ("v", g.vector.tensor_scalar),
           "cp": ("v", g.vector.tensor_copy), "ms": ("v", g.vector.memset), "scan": ("v", g.vector.tensor_tensor_scan),
           "act": ("s", g.scalar.activation), "iota": ("g", g.iota), "asel": ("g", g.affine_select)}

    def op(name, reads, writes, out, *args, acc=False, w=1.0, **kw):
        e, fn = fns[name]
        n = 1
        for s in out.shape[1:]:
            n *= int(s)
        if e == "p":
            cost = 0.0008 * max(64, n) * w
        elif e == "g":
            cost = 0.15 + 0.002 * n
        else:
            if name == "tt" and not any(k.split(":")[0] in BANKS for k in reads):
                w = max(w, 2.0)
            cost = 0.06 + 0.001 * n * w
        return add(e, reads, writes, lambda: fn(out, *args, **kw), "c" + e, 1, cost, acc=acc)

    def dma(e, reads, writes, sem, out, in_):
        return add(e, reads, writes, lambda: eng[e].dma_start(out, in_), sem, 16, 0.1, lag=4.0)

    def send(reads, transfers, n):
        return add("g", reads, [], lambda: g.remote_dma_fused(transfers, local_sem=T.sem.loc), "loc", n, 1.0, own=False)

    def arrives(sem, n, writes, sent, lag):
        add("x", [], writes, None, sem, n, 0.0, lag=lag, after=[sent])

    def finish():
        n = len(nodes)
        succ = [[] for _ in range(n)]
        for k, x in enumerate(nodes):
            x["all"] = sorted(set(x["deps"] + ([x["prev"]] if "prev" in x else [])))
            for d in x["all"]:
                succ[d].append(k)
        prio = [0.0] * n
        for k in range(n - 1, -1, -1):
            x = nodes[k]
            prio[k] = x["cost"] + max([prio[s] + (0.0 if nodes[s].get("prev") == k else x["lag"]) for s in succ[k]] + [0.0])
        left = [len(x["all"]) for x in nodes]
        ready = {e: [] for e in "vspgyx"}
        free = {e: 0.0 for e in "vspgyx"}
        start = [0.0] * n
        for k in range(n):
            if not left[k]:
                ready[nodes[k]["e"]].append(k)
        order = []
        while len(order) < n:
            best = None
            for e, lst in ready.items():
                if lst:
                    t = min(start[k] for k in lst)
                    t = t if e == "x" else max(free[e], t)
                    if best is None or t < best[0]:
                        best = (t, e)
            t, e = best
            k = max((k for k in ready[e] if start[k] <= t + 1e-9), key=lambda k: (prio[k], -k))
            ready[e].remove(k)
            order.append(k)
            x = nodes[k]
            free[e] = t + x["cost"]
            for s in succ[k]:
                start[s] = max(start[s], t + x["cost"] + (0.0 if nodes[s].get("prev") == k else x["lag"]))
                left[s] -= 1
                if not left[s]:
                    ready[nodes[s]["e"]].append(s)
        cnt, known, event, clock = {}, {e: {} for e in eng}, {}, {}
        for k in order:
            x = nodes[k]
            e = x["e"]
            if e == "x":
                event[k] = (x["sem"], x["inc"])
                clock[event[k]] = {x["sem"]: x["inc"]}
                continue
            need = {}
            for d in x["deps"]:
                s, m = event[d]
                need[s] = max(need.get(s, 0), m)
            todo = [(s, m) for s, m in need.items() if known[e].get(s, 0) < m]
            todo = [p for p in todo if not any(q != p and clock[q].get(p[0], 0) >= p[1] for q in todo)]
            for p in todo:
                eng[e].wait_ge(T.sem[p[0]], p[1])
                for s, m in clock[p].items():
                    known[e][s] = max(known[e].get(s, 0), m)
            ins = x["emit"]()
            cnt[x["sem"]] = cnt.get(x["sem"], 0) + x["inc"]
            if x["own"]:
                ins.then_inc(T.sem[x["sem"]], x["inc"])
            event[k] = (x["sem"], cnt[x["sem"]])
            clock[event[k]] = dict(known[e])
            clock[event[k]][x["sem"]] = cnt[x["sem"]]
        for s, m in cnt.items():
            if known["g"].get(s, 0) < m:
                g.wait_ge(T.sem[s], m)

    return op, dma, send, arrives, finish


def rank_program(g, core, T, topo):
    rank = T.rank_of(core)
    if rank is None:
        return
    op, dma, send, arrives, finish = make_plan(g, T)
    peers = [c for c in T.cores if c != core]
    nxt = T.cores[(rank + STEP) % NR]
    efl = [e for e in topo.engines(core, peers[0]) if all(e in topo.engines(core, c) for c in peers)]
    enx = topo.engines(core, nxt)
    hn = len(enx) // 2

    def to(c):
        return DstId(rid=topo.addr(c)[0], pnc=topo.addr(c)[1])

    def bits(es):
        return sum(1 << e for e in es)

    TXK = ["TX.%d" % j for j in range(6)]
    X0 = ["LX0.%d" % j for j in range(3)]

    def cs(n, r=0):
        return slice(V * r + 128 * n, V * r + 128 * n + 128)

    dma("y", [], ["PI"], "d0", T.PI[:], T.p0[:])
    dma("y", [], X0, "d1", T.LX0[:], T.x0[:])
    for j in range(3):
        dma("y", [], TXK[2 * j:2 * j + 2], "d%d" % (2 + j), T.TX[:, 1024 * j:1024 * j + 1024], T.tx[:, 1024 * j:1024 * j + 1024])
    dma("y", [], ["PU"], "d5", T.PU[:], T.pu[:])
    lo = {"allow_small_or_imprecise_dtypes": True}
    op("ms", [], ["ONE"], T.ONE[:], 1.0)
    op("asel", ["ONE"], ["IDB"], T.IDB[:], T.ONE[:, 0:128], [[-1, 128]], A.is_equal, 0.0, 0, 1)
    op("asel", ["ONE"], ["BO"], T.BO[:], T.ONE[:, 0:128], [[-16, 8], [0, 16]], A.is_ge, 0.0, 0, 1)
    op("asel", ["BO"], ["BO"], T.BO[:], T.BO[:], [[16, 8], [0, 16]], A.is_ge, 0.0, 15, -1)
    op("ms", [], ["TRI"], T.TRI[:], 0.0)
    op("cp", ["BO"], ["TRI"], T.TRI[:, :, 0:16], T.BO[:])
    op("asel", ["TRI"], ["TRI"], T.TRI[:], T.TRI[:], [[16, 8], [1, 32]], A.is_ge, 0.0, -1, -1)
    op("ms", [], ["TRI"], T.TRI[:, :, 0:2], 0.0)
    op("ms", [], ["XT"], T.XT[:], 0.0)
    op("ts", ["BO"], ["XT"], T.XT[:, :, 0:16], T.BO[:], 64.0, None, A.mult)
    op("ms", [], ["CP"], T.CP[:], 0.0)
    op("ms", [], ["CP"], T.CP[:, :, 16:32], 1.0)
    op("ms", [], ["ZER"], T.ZER[:], 0.0)
    for n, c in (("RSK", BIG), ("RSE", -BIG)):
        op("ms", [], [n], T[n][:], 0.0)
        op("ms", [], [n], T[n][:, 0:256:32], c)
    for j in range(3):
        for n, k in (("OF", 128), ("OK", 128), ("SC", 256), ("SK", 256)):
            n += "%d" % j
            op("ms", [], [n + ".e"], T[n][:, k:k + (8 if k == 128 else 16)], 0.0)
        op("ms", [], ["PM%d.e" % j], T["PM%d" % j][:, 255:256], 1.0)
    op("cp", ["PI"], ["LP0.0", "LP0.1", "LP0.2"], T.LP0[:], T.PI[:])
    op("cp", ["PI"], ["PF0.0", "PF0.1", "PF0.2"], T.PF0[:], T.PI[:])
    op("ts", X0, X0, T.LX0[:], T.LX0[:], 128.0, None, A.add)
    for j in range(6):
        c = slice(512 * j, 512 * j + 512)
        if j % 2 == 0:
            op("ts", [TXK[j]], [TXK[j]], T.TX[:, c], T.TX[:, c], 128.0, None, A.add, w=0.5)
        else:
            op("act", [TXK[j]], [TXK[j]], T.TX[:, c], T.TX[:, c], F.Identity, bias=128.0)
    op("ts", ["BO"], ["BM"], T.BM[:], T.BO[:, 0:128:16], -64.0, None, A.mult)
    op("ts", ["BO"], ["BG"], T.BG[:], T.BO[:, 0:128:16], 32.0, None, A.mult)
    op("cp", ["BO"], ["BOF"], T.BOF[:], T.BO[:])
    op("iota", [], ["CK"], T.CK[:], [[0, 8], [1, 32]], -15, 0, **lo)
    op("ms", [], ["CK"], T.CK[:, :, 16:32], BIG)
    op("ms", [], ["CK"], T.CK[:, :, 0:1], 131072.0)
    op("iota", [], ["IOM"], T.IOM[:], [[1, 128]], 0, 0, **lo)
    op("iota", [], ["IOL"], T.IOL[:], [[128, 24]], 0, 0, **lo)
    op("iota", [], ["IOI"], T.IOI[:], [[1, 128]], 0, -1)
    op("iota", [], ["CE"], T.CE[:], [[0, 8], [-1, 32]], -17, 0, **lo)
    op("asel", ["ONE"], ["EX"], T.EX[:], T.ONE[:], [[-1, 12], [-12, 8], [0, 16]], A.is_equal, 0.0, 0, 1)
    op("ts", ["IOI"], ["IOI"], T.IOI[:], T.IOI[:], 15, None, A.bitwise_and)
    op("ts", ["IOI"], ["MASK"], T.MASK[:], T.IOI[:], 0.0, None, A.is_equal)
    op("cp", ["IDB"], ["IDF"], T.IDF[:], T.IDB[:])
    op("ts", ["IDB"], ["IDH"], T.IDH[:], T.IDB[:], 0.5, None, A.mult)
    op("ts", ["BO"], ["BO4"], T.BO4[:], T.BO[:], 4096.0, None, A.mult)
    op("ms", [], ["CE"], T.CE[:, :, 16:32], -BIG)
    op("ms", [], ["CE"], T.CE[:, :, 16:17], 0.0)

    def mm(reads, writes, out, lhsT, rhs, start, stop, w=1.0):
        return op("mm", reads, writes, out, lhsT, rhs, start, stop, acc=not start, w=w)

    def distances(p, r, n, lists, lkey):
        K, M, XR, X, G = T["K%d" % (p % 3)], T["M%d" % (p % 2)], T["XR%d" % (p % 2)], T["LX%d" % r][:, cs(n)], T["G%d" % (p % NG)]
        kk, mk, xr, xk, gk = "K%d:k" % (p % 3), "M%d." % (p % 2), "XR%d:" % (p % 2), "LX%d.%d" % (r, n), "G%d." % (p % NG)
        mm([xk, "XT"], [kk], K[:, 0:256], X, T.XT[:], True, False)
        for j in range(4):
            mm(["IDB", xk], [xr + "%d" % j], XR[:, j::4], T.IDB[:], X, True, True)
        for h in range(2):
            op("act", TXK + [lkey], [gk + "%d" % h], G[:, 1024 * h:1024 * h + 1024],
               T.TX[:, 0:W].indirect(lists[:, 128 * n + 64 * h:128 * n + 64 * h + 64]), F.Copy, w=1.5)
        for k in range(16):
            mm([gk + "0", gk + "1", "BG"], [kk], K[:, k:256:32], G[:, k::16], T.BG[:], False, False)
        for h in range(2):
            for j in range(4):
                c = slice(1024 * h + j, 1024 * h + 1024, 4)
                op("tt", [gk + "%d" % h] + [xr + "%d" % q for q in range(4)], [mk + "%d.%d" % (h, j)], M[:, c], G[:, c],
                   XR[:, 256 * h:256 * h + 256], A.max)
        for k in (0, 4, 8, 12, 1, 5, 9, 13, 2, 6, 10, 14, 3, 7, 11, 15):
            mm([mk + "%d.%d" % (h, k % 4) for h in range(2)] + ["BM"], [kk], K[:, k:256:32], M[:, k::16], T.BM[:], False, False)

    def one_hot(z, src, skey, dz, S, O, minmax):
        op("scan", [skey, dz], [S], T[S][:, 0:256], T[dz][:], src, 0.0, A.add, minmax)
        op("tt", [skey, S, S + ".e"], ["OT" + z], T["OT" + z][:], src, T[S][:, 16:272], A.is_equal)
        op("cp", ["OT" + z], [O], T[O][:, 0:128], T["OT" + z][:, :, 0:16], w=0.5)

    def to_list(y):
        op("tt", ["PB:r", "MASK"], ["MK" + y], T["MK" + y][:], T.PB[:, 128:256], T.MASK[:], A.mult)
        mm(["MK" + y, "BOF"], ["PB:l"], T.PB[:, 256:264], T["MK" + y][:], T.BOF[:, 0:128:16], True, True, w=4)
        op("cp", ["PB:l"], ["PL" + y], T["PL" + y][:], T.PB[:, 256:264])

    def first_half(r, n, p):
        z, y = "%d" % (p % 3), "%d" % (p % 2)
        PF, pfk, pk = T["PF%d" % (r % 2)], "PF%d.%d" % (r % 2, n), "LP%d.%d" % (r, n)
        K, kk, ck = T["K" + z], "K%s:k" % z, "K%s:c" % z
        if r:
            op("cp", [pk], [pfk], PF[:, cs(n)], T["LP%d" % r][:, cs(n)])
        for j in range(2):
            op("tt", [pfk], ["DF%s.%d" % (z, j)], T["DF" + z][:, j:128:2], PF[:, 128 * n:128 * n + 128:2], PF[:, 128 * n + 1:128 * n + 128:2],
               A.not_equal)
        mm(["DF%s.0" % z, "DF%s.1" % z, "TRI"], [ck], K[:, 256:512], T["DF" + z][:], T.TRI[:], True, False)
        mm(["IDB", "CP"], [ck], K[:, 256:512], T.IDB[:], T.CP[:], False, True)
        op("act", [ck], ["DZ" + z], T["DZ" + z][:], K[:, 256:512], F.Relu, bias=BIG, scale=-BIG)
        if r:
            op("act", ["DZ" + z], ["PM" + z], T["PM" + z][:, 0:255], T["DZ" + z][:, 1:256], F.Identity, bias=1.0 / 1024, scale=1.0 / BIG)
        distances(p, r, n, T["LP%d" % r], pk)
        mm(["IDB", "CK"], [kk], K[:, 0:256], T.IDB[:], T.CK[:], False, True)
        one_hot(z, K[:, 0:256], kk, "DZ" + z, "SC" + z, "OF" + z, A.min)
        mm(["OF" + z, "IDB"], ["PA:n"], T.PA[:, 0:128], T["OF" + z][:, 0:128], T.IDB[:], True, True)
        op("tt", ["PA:n", pfk], ["SP" + y], T["SP" + y][:], T.PA[:, 0:128], PF[:, cs(n)], A.mult)
        mm(["SP" + y, "BOF"], ["PA:c"], T.PA[:, 128:136], T["SP" + y][:], T.BOF[:, 0:128:16], True, True, w=4)
        op("cp", ["PA:c"], ["CI" + y], T["CI" + y][:], T.PA[:, 128:136])
        op("act", ["PA:c"], ["LB" + y], T["LB" + y][:], T.PA[:, 128:136], F.Identity, bias=63.5, scale=-1.0)
        op("ts", ["CI" + y], ["CI" + y], T["CI" + y][:], T["CI" + y][:], 127, None, A.bitwise_and)
        for j in range(8):
            op("act", ["LB" + y, "IOL"], ["OL%s.%d" % (y, j)], T["OL" + y][:, j, :], T.IOL[:], F.Abs, bias=T["LB" + y][:, j:j + 1])
        op("cp", ["CI" + y], ["CF" + y], T["CF" + y][:], T["CI" + y][:])
        op("act", ["OL%s.%d" % (y, j) for j in range(8)], ["OM" + y], T["OM" + y][:], T["OL" + y][:], F.Relu, bias=64.5, scale=-1.0)
        for j in range(8):
            op("ts", ["CF" + y, "IOM"], ["OH%s.%d" % (y, j)], T["OH" + y][:, j, :], T.IOM[:], T["CF" + y][:, j:j + 1], None, A.is_equal, w=0.5)
        for j in range(8):
            mm(["OH%s.%d" % (y, j), "OM" + y], ["HI:h"], T.HI[:, j, 0:24], T["OH" + y][:, j, :], T["OM" + y][:, j, :], False, False)
        if n == 2:
            spread(r)
        th, tc = "TH%d" % n, T.TH[:, 8 * n:8 * n + 8]
        if r == 0:
            O = "OF" + z
            op("ts", ["SC" + z], [th], tc, T["SC" + z][:, 31:256:32], -15.0, None, A.max)
        else:
            O = "OK" + z
            op("tt", [kk, "PM" + z, "PM%s.e" % z], ["AJ" + z], T["AJ" + z][:], K[:, 0:256], T["PM" + z][:], A.mult)
            one_hot(z, T["AJ" + z][:], "AJ" + z, "RSK", "SK" + z, O, A.min)
            op("ts", ["SK" + z], [th], tc, T["SK" + z][:, 31:256:32], -15.0 / 1024, 1024.0, A.max, A.mult)
        mm([O, O + ".e", "IDB"], ["PB:n"], T.PB[:, 0:128], T[O][:, 1:129], T.IDB[:], True, True)
        mm([O, "IDB"], ["PB:o"], T.PB[:, 384:512], T[O][:, 0:128], T.IDB[:], True, True)
        op("tt", ["PB:n", pfk], ["SQ" + y], T["SQ" + y][:], T.PB[:, 0:128], PF[:, cs(n)], A.mult)
        op("act", ["PB:o"], ["ONK.%d" % n], T.ONK[:, cs(n)], T.PB[:, 384:512], F.Copy)
        mm(["SQ" + y, "BOF"], ["PB:r"], T.PB[:, 128:256], T["SQ" + y][:], T.BOF[:], True, True, w=4)
        to_list(y)
        op("cp", ["PL" + y, "PU"], ["CU.%d" % n], T.CU[:, cs(n)], T.PU[:, 0:W].indirect(T["PL" + y][:]), w=1.5)
        op("cp", ["CU.%d" % n], ["CD.%d" % n], T.CD[:, cs(n)], T.CU[:, cs(n)])

    def spread(r):
        mm(["ZER", "ONE"], ["HI:h"], T.HI[:], T.ZER[:], T.ONE[:, 0:192], False, True)
        pk, PK = "PK%d" % r, T.PK[:, 96 * r:96 * r + 96]
        op("ts", ["HI:h"], ["FA"], T.FA[:], T.HI[:, :, 0:12], 1.0, None, A.min)
        op("ts", ["HI:h"], ["FB"], T.FB[:], T.HI[:, :, 12:24], 1.0, 16.0, A.min, A.mult)
        op("tt", ["FA", "FB"], [pk], PK, T.FA[:], T.FB[:], A.add)
        s = send([pk], [RemoteDMATransfer(dst_ids=[to(c) for c in peers], dma_engine_mask=bits(efl), remote_sem=T.sem["fl%d" % r],
                                          srcs=[PK], dsts=[T["FL%d" % r][:, rank, :] for c in peers])], len(efl))
        arrives("fl%d" % r, 7 * len(efl), ["FL%d" % r], s, 6.0)

    def cuts(r):
        pk, fl, nc = "PK%d" % r, "FL%d" % r, "NC%d" % r
        cnt = T.PA[0:96, 0:128]
        others = [k for k in range(NR) if k != rank]
        mm([pk, "IDB"], ["PA:n"], cnt, T.PK[:, 96 * r:96 * r + 96], T.IDB[:], True, False)
        for k in others:
            mm([fl, "IDB"], ["PA:n"], cnt, T[fl][:, k, :], T.IDB[:], False, k == others[-1])
        op("cp", ["PA:n"], ["CNI"], T.CNI[0:96, :], cnt)
        op("ts", ["PA:n"], [nc + ".1"], T[nc][0:96, 1, :], cnt, 47.5, 256.0, A.is_lt, A.mult)
        op("ts", ["CNI"], ["CNI"], T.CNI[0:96, :], T.CNI[0:96, :], 15, None, A.bitwise_and)
        op("ts", ["CNI"], [nc + ".0"], T[nc][0:96, 0, :], T.CNI[0:96, :], 2.5, 256.0, A.is_lt, A.mult)
        banks = ("PB", "XR0", "XR1", "PA")
        for q, j in enumerate((3, 4, 5, 0, 1, 2)):
            bank, c = banks[q % len(banks)], slice(512 * j, 512 * j + 512)
            keys = [bank + ":%d" % l for l in range(4)]
            for l in range(4):
                L = 4 * j + l
                out = T[bank][:, 128 * l:128 * l + 128]
                if UPD[q]:
                    mm([TXK[j], "IDB"], [keys[l]], out, T.IDB[:], T.TX[:, 128 * L:128 * L + 128], True, False)
                mm([nc + ".%d" % (L // 12), "EX"], [keys[l]], out, T.EX[0:96, 128 * (L % 12):128 * (L % 12) + 128],
                   T[nc][0:96, L // 12, :], not UPD[q], True)
            if UPD[q]:
                op("act", keys, [TXK[j]], T.TX[:, c], T[bank][:], F.Relu, bias=-256.0)
            else:
                op("tt", keys + [TXK[j]], [TXK[j]], T.TX[:, c], T.TX[:, c], T[bank][:], A.min)

    def second_half(r, n, p):
        z, y, xk, x = "%d" % (p % 3), "%d" % (p % 2), "LX%d.%d" % (r, n), T["LX%d" % r][:, cs(n)]
        PF, pfk, oxk, opk = T["PF%d" % (r % 2)], "PF%d.%d" % (r % 2, n), "OX%d.%d" % (r, n), "OP%d.%d" % (r, n)
        K, kk = T["K" + z], "K%s:k" % z
        distances(p, r, n, T.CU, "CU.%d" % n)
        mm(["IDF", "TH%d" % n], [kk], K[:, 16:256:32], T.IDF[:], T.TH[:, 8 * n:8 * n + 8], False, False, w=4)
        mm(["IDB", "CE"], [kk], K[:, 0:256], T.IDB[:], T.CE[:], False, True)
        one_hot(z, K[:, 0:256], kk, "RSE", "SC" + z, "OF" + z, A.max)
        mm(["OF" + z, "IDB"], ["PA:n"], T.PA[:, 0:128], T["OF" + z][:, 0:128], T.IDB[:], True, True)
        op("tt", ["PA:n", "CD.%d" % n], ["SP" + y], T["SP" + y][:], T.PA[:, 0:128], T.CD[:, cs(n)], A.mult)
        op("act", ["PA:n"], ["OB" + y], T["OB" + y][:], T.PA[:, 0:128], F.Copy)
        mm(["SP" + y, "BOF"], ["PB:r"], T.PB[:, 128:256], T["SP" + y][:], T.BOF[:], True, True, w=4)
        mm(["OB" + y, "BO"], ["PB:n"], T.PB[:, 0:128], T.BO[:], T["OB" + y][:], True, True)
        mm(["SP" + y, "BOF"], ["PB:o"], T.PB[:, 384:512], T.BOF[:], T["SP" + y][:], True, False, w=4)
        mm(["OB" + y, "BO4"], ["PB:o"], T.PB[:, 384:512], T.BO4[:], T["OB" + y][:], False, True)
        to_list(y)
        op("tt", ["PL" + y, xk] + TXK, ["DX" + y], T["DX" + y][:], T.TX[:, 0:W].indirect(T["PL" + y][:]), x, A.subtract)
        op("tt", ["DX" + y, "PB:n"], ["DY" + y], T["DY" + y][:], T["DX" + y][:], T.PB[:, 0:128], A.mult)
        mm([xk, "IDB"], ["PA:x"], T.PA[:, 128:256], T.IDB[:], x, True, False)
        mm(["DY" + y, "IDH"], ["PA:x"], T.PA[:, 128:256], T.IDH[:], T["DY" + y][:], False, True)
        op("act", ["PA:x"], [oxk], T.OX[:, cs(n, r)], T.PA[:, 128:256], F.Identity, bias=-0.2)
        op("tt", ["ONK.%d" % n, "PB:o"], ["UU" + y], T["UU" + y][:], T.ONK[:, cs(n)], T.PB[:, 384:512], A.mult)
        op("tt", ["UU" + y, pfk], ["WI" + y], T["WI" + y][:], PF[:, cs(n)], T["UU" + y][:], A.max)
        op("ts", ["WI" + y], ["WI" + y], T["WI" + y][:], T["WI" + y][:], 4095, None, A.bitwise_and)
        if r < RO - 1:
            op("cp", ["WI" + y], [opk], T.OP[:, cs(n, r)], T["WI" + y][:])
            sem = T.sem["a%d%d" % (r, n)]
            s = send([oxk, opk], [
                RemoteDMATransfer(dst_ids=[to(nxt)], dma_engine_mask=bits(es), remote_sem=sem, src=T[o][:, cs(n, r)],
                                  dst=T["%s%d" % (l, r + 1)][:, cs(n)])
                for es, o, l in ((enx[:hn], "OP", "LP"), (enx[hn:], "OX", "LX"))], 2 * hn)
            arrives("a%d%d" % (r, n), 2 * hn, ["LP%d.%d" % (r + 1, n), "LX%d.%d" % (r + 1, n)], s, 4.0)
        else:
            op("cp", ["WI" + y], ["YP.%d" % n], T.YP[:, cs(n)], T["WI" + y][:])
            op("act", [oxk], ["YX.%d" % n], T.YX[:, cs(n)], T.OX[:, cs(n, r)], F.Identity, bias=-128.0)
            dma("y", ["YP.%d" % n], [], "d%d" % (6 + n), T.yp[:, cs(n)], T.YP[:, cs(n)])
            dma("y", ["YX.%d" % n], [], "d%d" % (9 + n), T.yx[:, cs(n)], T.YX[:, cs(n)])

    for r in range(RO):
        p = 6 * r
        mm(["ZER", "ONE"], ["HI:h"], T.HI[:], T.ZER[:], T.ONE[:, 0:192], True, False)
        for n in range(3):
            first_half(r, n, p + n)
        cuts(r)
        for n in range(3):
            second_half(r, n, p + 3 + n)
        if r == RO - 1:
            k = ["NC%d.%d" % (q, j) for q in range(RO) for j in range(2)]
            op("tt", k[0:4], ["YCA"], T.YCA[0:96], T.NC0[0:96], T.NC1[0:96], A.min)
            op("tt", ["YCA"] + k[4:6], ["YCA"], T.YCA[0:96], T.YCA[0:96], T.NC2[0:96], A.min)
            op("ts", ["YCA"], ["YC"], T.YC[0:96], T.YCA[0:96], 128.0, None, A.is_lt)
            for j in range(2):
                dma("y", ["YC"], [], "d%d" % (12 + j), T.yc[:, 1536 * j:1536 * j + 1536], T.YC[0:96, j, :])
    finish()
